import numpy as np
import ml_dtypes


def mxq(x, axis, fmt="e4m3"):
    dtype, down = {"e4m3": (ml_dtypes.float8_e4m3fn, 7), "e5m2": (ml_dtypes.float8_e5m2, 14)}[fmt]
    v = np.moveaxis(np.asarray(x, np.float32).astype(ml_dtypes.bfloat16).astype(np.float64), axis, -1)
    blocks = v.reshape(v.shape[:-1] + (-1, 32))
    amax = np.abs(blocks).max(-1, keepdims=True)
    byte = np.maximum(np.where(amax > 0, np.frexp(amax)[1] - 1 + 127, 0) - down, 1)
    scale = np.exp2(byte - 127.0)
    codes = (blocks / scale).astype(np.float32).astype(dtype).astype(np.float64)
    return np.moveaxis((codes * scale).reshape(v.shape), -1, axis)


WIDE = False


def mx_kscale(k):
    if not WIDE:
        return np.ones(k)
    levels = np.array([10, -10, 5, -5, 0])
    if k % 512:
        return np.exp2(np.random.permutation(np.resize(levels, k // 32))).repeat(32)
    a = np.empty((k // 512, 16))
    for p in range(k // 512):
        a[p, :8] = np.random.permutation(np.resize(levels, 8))
        for g in range(8):
            far = levels[np.abs(levels - a[p, g]) >= 10]
            a[p, g + 8] = far[np.random.randint(len(far))]
    return np.exp2(a.ravel()).repeat(32)


BF16 = ml_dtypes.bfloat16


def bf(x):
    return np.asarray(x, np.float32).astype(BF16)


def f64(x):
    return np.asarray(x).astype(np.float64)


E2M1 = np.array([0.0, 0.5, 1.0, 1.5, 2.0, 3.0, 4.0, 6.0, -0.0, -0.5, -1.0, -1.5, -2.0, -3.0, -4.0, -6.0])


def pack_weight(w, fmt):
    k, n = w.shape
    w = f64(bf(w)).reshape(k // 32, 32, n)
    amax = np.abs(w).max(1)
    if fmt == "e4m3":
        byte = np.frexp(amax)[1] - 1 + 127 - 7
    else:
        mant, ex = np.frexp(amax / 6.0)
        byte = np.where(mant > 0.5, ex, ex - 1) + 127
    byte = np.clip(np.where(amax > 0, byte, 1), 1, 254)
    scaled = (w * np.exp2(127.0 - byte)[:, None, :]).reshape(k, n).astype(np.float32)
    by_word = np.ascontiguousarray(scaled.reshape(k // 512, 128, 4, n).transpose(0, 1, 3, 2))
    if fmt == "e4m3":
        words = by_word.astype(ml_dtypes.float8_e4m3fn).view(np.uint8)
    else:
        c = by_word.astype(ml_dtypes.float4_e2m1fn).view(np.uint8) & 0xF
        words = c[..., 0::2] | (c[..., 1::2] << 4)
    return np.ascontiguousarray(words), np.ascontiguousarray(byte.astype(np.uint8).reshape(k // 512, 16, n))


def unpack_weight(words, scales, fmt):
    g, p, n, _ = words.shape
    if fmt == "e4m3":
        vals = np.ascontiguousarray(words).view(ml_dtypes.float8_e4m3fn).astype(np.float64)
    else:
        nib = np.empty((g, p, n, 4), np.uint8)
        nib[..., 0::2] = words & 0xF
        nib[..., 1::2] = words >> 4
        vals = E2M1[nib]
    vals = vals * np.repeat(np.exp2(scales.astype(np.float64) - 127.0), 8, axis=1)[..., None]
    return vals.transpose(0, 1, 3, 2).reshape(g * 512, n)
def pack4(w):
    words, scales = pack_weight(w, "e2m1")
    return words.reshape(words.shape[0], 128, -1), scales


def unpack4(words, scales):
    return unpack_weight(words.reshape(words.shape[0], 128, -1, 2), scales, "e2m1")


M, K, S, D = 2048, 1024, 1536, 512
SPREAD = 1.75


def setup_inputs():
    s = mx_kscale(K)
    t = mx_kscale(S)
    plans = np.exp(SPREAD * np.random.standard_normal((K, M)))
    lognon = -np.exp(SPREAD * np.random.standard_normal((K, S)) - SPREAD ** 2) / K
    demo = np.random.standard_normal((S, D)) / np.sqrt(S)
    plans_words, plans_scales = pack4(plans * s[:, None])
    lognon_words, lognon_scales = pack4(lognon / s[:, None])
    demo_words, demo_scales = pack_weight(demo / t[:, None], "e4m3")
    return {"plans_words": plans_words, "plans_scales": plans_scales,
            "lognon_words": lognon_words, "lognon_scales": lognon_scales,
            "audience": bf(np.exp(0.4 * np.random.standard_normal(S)) * t),
            "demo_words": demo_words, "demo_scales": demo_scales}


def reference(plans_words, plans_scales, lognon_words, lognon_scales, audience, demo_words, demo_scales):
    a = unpack4(plans_words, plans_scales)
    l = unpack4(lognon_words, lognon_scales)
    z = a.T @ l
    reach = 1.0 - np.exp(z)
    h = reach * f64(audience)
    w = unpack_weight(demo_words, demo_scales, "e4m3")
    return mxq(h, 1, "e4m3") @ w

@@ -1,0 +1,227 @@
+from contextlib import ExitStack
+
+import concourse.mybir as mybir
+
+M, K, S, D = 2048, 1024, 1536, 512
+FLOPS = 2 * M * K * S + 2 * M * S * D
+
+F32 = mybir.dt.float32
+BF16 = mybir.dt.bfloat16
+I32 = mybir.dt.int32
+U8 = mybir.dt.uint8
+FP8X4 = mybir.dt.float8_e4m3fn_x4
+FP4X4 = mybir.dt.float4_e2m1fn_x4
+ACT = mybir.ActivationFunctionType
+ALU = mybir.AluOpType
+
+P = 128
+PACK = 4
+W = 512
+KG = K // W
+SG = S // W
+MB = M // W
+UNITS = MB * SG
+STEPS = UNITS * PACK
+TILES = M // P
+Z_BANKS = 6
+FIRST_OUT = 23
+OUT_EVERY = 3
+E_BUFS = 16
+
+
+def tile_campaign_reach_by_demographic_s4_kernel(
+    tc, plans_words, plans_scales, lognon_words, lognon_scales, audience, demo_words, demo_scales, out
+):
+    nc = tc.nc
+    with ExitStack() as ctx:
+        keep = ctx.enter_context(tc.tile_pool(name="keep", bufs=1))
+        work = ctx.enter_context(tc.tile_pool(name="work", bufs=1))
+        psum = ctx.enter_context(tc.psum_pool(name="psum", bufs=1))
+        ctx.enter_context(tc.manual_schedule())
+
+        def kept(name, shape, dtype):
+            return keep.tile(shape, dtype, name=name, align_bytes=256)
+
+        def plane(name, groups, width):
+            t = kept(name, [P, groups, width], U8)
+            nc.vector.memset(t[:].rearrange("p g n -> p (g n)").bitcast(I32), 0)
+            return t
+
+        def load_scales(t, scales, col0, width, quads=range(4)):
+            for q in quads:
+                src = scales[:, 4 * q : 4 * q + 4, col0 : col0 + width].rearrange("g r n -> r g n")
+                nc.sync.dma_start(out=t[32 * q : 32 * q + 4, :, :].bitcast(I32), in_=src.bitcast(I32))
+
+        def load_fp4(name, words, j):
+            t = kept(name, [P, KG, 2 * W], U8)
+            src = words[:, :, 2 * W * j : 2 * W * (j + 1)].rearrange("g p n -> p g n")
+            nc.sync.dma_start(out=t[:].bitcast(I32), in_=src.bitcast(I32))
+            return t
+
+        warm = kept("warm", [P, 8], F32)
+        ls_first = plane("ls_first", KG, W)
+        as_first = plane("as_first", KG, W)
+        nc.vector.memset(warm[:, 0:1], 0.0)
+        nc.scalar.activation(out=warm[:, 4:5], in_=warm[:, 0:1], func=ACT.Exp)
+        ls_rest = plane("ls_rest", KG, S - W)
+        as_rest = plane("as_rest", KG, M - W)
+        d_scales = plane("d_scales", SG, D)
+
+        load_scales(ls_first, lognon_scales, 0, W, range(0, 2))
+        l_raw = [load_fp4("l_raw0", lognon_words, 0)]
+        a_codes = [load_fp4("a_codes0", plans_words, 0)]
+        load_scales(ls_first, lognon_scales, 0, W, range(2, 4))
+        load_scales(as_first, plans_scales, 0, W)
+        l_raw.append(load_fp4("l_raw1", lognon_words, 1))
+        load_scales(ls_rest, lognon_scales, W, S - W)
+        l_raw.append(load_fp4("l_raw2", lognon_words, 2))
+        aud = kept("aud", [P, SG, PACK], BF16)
+        nc.sync.dma_start(out=aud[:], in_=audience.rearrange("(g p t) -> p g t", p=P, t=PACK))
+        load_scales(as_rest, plans_scales, W, M - W)
+        a_codes.append(load_fp4("a_codes1", plans_words, 1))
+        load_scales(d_scales, demo_scales, 0, D)
+        d_codes = kept("d_codes", [P, SG, D], I32)
+        nc.sync.dma_start(out=d_codes[:], in_=demo_words.rearrange("g p n t -> p g (n t)").bitcast(I32))
+        for j in range(2, MB):
+            a_codes.append(load_fp4("a_codes%d" % j, plans_words, j))
+
+        l_codes = [kept("l_codes%d" % g, [P, PACK, KG, 2 * P], U8) for g in range(SG)]
+        l_scales = [kept("l_scales%d" % g, [P, PACK, KG, P], U8) for g in range(SG)]
+
+        def sort_codes(g, t0, t1):
+            src = l_raw[g][:].rearrange("p k (m t b) -> p t k m b", t=PACK, b=2)
+            dst = l_codes[g][:].rearrange("p t k (m b) -> p t k m b", b=2)
+            nc.vector.tensor_copy(out=dst[:, t0:t1], in_=src[:, t0:t1])
+
+        def sort_scales(g, t0, t1):
+            raw = ls_first[:] if g == 0 else ls_rest[:, :, W * (g - 1) : W * g]
+            src = raw.rearrange("p k (m t) -> p t k m", t=PACK)
+            nc.vector.tensor_copy(out=l_scales[g][:, t0:t1], in_=src[:, t0:t1])
+
+        sort_codes(0, 0, 1)
+        sort_scales(0, 0, 2)
+        sort_codes(0, 1, 2)
+        sort_scales(0, 2, 4)
+        sort_codes(0, 2, 4)
+        for g in range(1, SG):
+            sort_codes(g, 0, PACK)
+            sort_scales(g, 0, PACK)
+        neg_aud = kept("neg_aud", [P, SG, PACK], F32)
+        nc.vector.tensor_scalar(out=neg_aud[:], in0=aud[:], scalar1=-1.0, scalar2=None, op0=ALU.mult)
+        pos_aud = kept("pos_aud", [P, PACK * SG], F32)[:].rearrange("p (g t) -> p g t", t=PACK)
+        nc.vector.tensor_copy(out=pos_aud, in_=aud[:])
+
+        h_codes = [kept("h_codes%d" % u, [P, W], I32) for u in range(UNITS)]
+        h_scales = [kept("h_scales%d" % u, [P, W], U8) for u in range(UNITS)]
+        missed = {}
+        h_slots = {}
+        h_words = {}
+        open_out = {}
+
+        def bank(b):
+            return psum.tile([P, W], F32, name="bank%d" % b, tag="bank%d" % b)
+
+        def reach(i):
+            u, t = divmod(i, PACK)
+            mb, g = divmod(u, SG)
+            z = bank(i % Z_BANKS)
+            for k in range(KG):
+                a_scale = as_first[:, k, :] if mb == 0 else as_rest[:, k, W * (mb - 1) : W * mb]
+                nc.tensor.matmul_mx(
+                    out=z[:],
+                    lhsT=l_codes[g][:, t, k, :].bitcast(FP4X4),
+                    lhsT_scale=l_scales[g][:, t, k, :],
+                    rhs=a_codes[mb][:, k, :].bitcast(FP4X4),
+                    rhs_scale=a_scale,
+                    start=(k == 0),
+                    stop=(k == KG - 1),
+                )
+            e = work.tile([P, W], F32, name="e", tag="e", bufs=E_BUFS)
+            nc.scalar.activation(out=e[:], in_=z[:], func=ACT.Exp)
+            missed[i] = e
+
+        def weigh(i, on_scalar):
+            u, t = divmod(i, PACK)
+            g = u % SG
+            if t == 0:
+                h_slots[u] = work.tile([P, PACK, W], BF16, name="h_slot", tag="h_slot", bufs=2, align_bytes=256)
+            if on_scalar:
+                nc.scalar.activation(
+                    out=h_slots[u][:, t, :], in_=missed[i][:], func=ACT.Identity,
+                    scale=neg_aud[:, g, t : t + 1], bias=pos_aud[:, g, t : t + 1],
+                )
+            else:
+                nc.vector.tensor_scalar(
+                    out=h_slots[u][:, t, :], in0=missed[i][:], scalar1=-1.0, scalar2=neg_aud[:, g, t : t + 1],
+                    op0=ALU.add, op1=ALU.mult,
+                )
+
+        def interleave(u, c0, c1):
+            if c0 == 0:
+                h_words[u] = work.tile([P, W, PACK], BF16, name="h_word", tag="h_word", bufs=2, align_bytes=256)
+            nc.vector.tensor_copy(
+                out=h_words[u][:, c0:c1, :].rearrange("p (c i) t -> p c t i", i=4),
+                in_=h_slots[u][:, :, c0:c1].rearrange("p t (c i) -> p c t i", i=4),
+            )
+
+        def quantize(u, c0, c1):
+            nc.vector.quantize_mx(
+                out=h_codes[u][:, c0:c1].bitcast(FP8X4),
+                scales=h_scales[u][:, c0:c1],
+                in_=h_words[u][:, c0:c1, :].rearrange("p c t -> p (c t)"),
+            )
+
+        def out_passes(j, b, g0, g1):
+            mb, c = divmod(j, W // P)
+            if g0 == 0:
+                open_out[j] = bank(b)
+            for g in range(g0, g1):
+                u = mb * SG + g
+                nc.tensor.matmul_mx(
+                    out=open_out[j][:],
+                    lhsT=h_codes[u][:, P * c : P * (c + 1)].bitcast(FP8X4),
+                    lhsT_scale=h_scales[u][:, P * c : P * (c + 1)],
+                    rhs=d_codes[:, g, :].bitcast(FP8X4),
+                    rhs_scale=d_scales[:, g, :],
+                    start=(g == 0),
+                    stop=(g == SG - 1),
+                )
+
+        def out_store(j, on_vector):
+            res = work.tile([P, D], F32, name="res", tag="res", bufs=4)
+            if on_vector:
+                nc.vector.tensor_copy(out=res[:], in_=open_out[j][:])
+            else:
+                nc.scalar.copy(out=res[:], in_=open_out[j][:])
+            nc.sync.dma_start(out=out[P * j : P * (j + 1), :], in_=res[:])
+
+        done = 0
+        for i in range(STEPS):
+            u, t = divmod(i, PACK)
+            reach(i)
+            if u < UNITS - 1:
+                weigh(i, False)
+            if u > 0 and t == 0:
+                interleave(u - 1, 0, W)
+            if u > 0 and t == 1:
+                quantize(u - 1, 0, W)
+            if i >= FIRST_OUT and (i - FIRST_OUT) % OUT_EVERY == 0 and i < STEPS - 1:
+                out_passes(done, Z_BANKS + done % 2, 0, SG)
+                out_store(done, False)
+                done = done + 1
+        for i in range(STEPS - PACK, STEPS):
+            weigh(i, True)
+        last = TILES - W // P
+        for j in range(done, last):
+            out_passes(j, Z_BANKS + j % 2, 0, SG)
+            out_store(j, False)
+        for j in range(last, TILES):
+            out_passes(j, j - last, 0, SG - 1)
+        interleave(UNITS - 1, 0, P)
+        for c in range(W // P):
+            if c + 1 < W // P:
+                interleave(UNITS - 1, P * (c + 1), P * (c + 2))
+            quantize(UNITS - 1, P * c, P * (c + 1))
+            out_passes(last + c, c, SG - 1, SG)
+        for j in range(last, TILES):
+            out_store(j, j == TILES - 1)

@@ -24,9 +24,14 @@ UNITS = MB * SG
 STEPS = UNITS * PACK
 TILES = M // P
 Z_BANKS = 6
-FIRST_OUT = 23
+FIRST_OUT = 32
 OUT_EVERY = 3
-E_BUFS = 16
+E_BUFS = 20
+WARM = 2
+ON_SCALAR = 4
+LEAD = 2
+RATE = 2
+QT = 3
 
 
 def tile_campaign_reach_by_demographic_s4_kernel(
@@ -67,11 +72,11 @@ def tile_campaign_reach_by_demographic_s4_kernel(
         as_rest = plane("as_rest", KG, M - W)
         d_scales = plane("d_scales", SG, D)
 
-        load_scales(ls_first, lognon_scales, 0, W, range(0, 2))
+        load_scales(ls_first, lognon_scales, 0, W)
         l_raw = [load_fp4("l_raw0", lognon_words, 0)]
+        load_scales(as_first, plans_scales, 0, W, range(0, 2))
         a_codes = [load_fp4("a_codes0", plans_words, 0)]
-        load_scales(ls_first, lognon_scales, 0, W, range(2, 4))
-        load_scales(as_first, plans_scales, 0, W)
+        load_scales(as_first, plans_scales, 0, W, range(2, 4))
         l_raw.append(load_fp4("l_raw1", lognon_words, 1))
         load_scales(ls_rest, lognon_scales, W, S - W)
         l_raw.append(load_fp4("l_raw2", lognon_words, 2))
@@ -98,28 +103,40 @@ def tile_campaign_reach_by_demographic_s4_kernel(
             src = raw.rearrange("p k (m t) -> p t k m", t=PACK)
             nc.vector.tensor_copy(out=l_scales[g][:, t0:t1], in_=src[:, t0:t1])
 
+        sort_scales(0, 0, PACK)
         sort_codes(0, 0, 1)
-        sort_scales(0, 0, 2)
         sort_codes(0, 1, 2)
-        sort_scales(0, 2, 4)
         sort_codes(0, 2, 4)
         for g in range(1, SG):
-            sort_codes(g, 0, PACK)
+            sort_codes(g, 0, 2)
             sort_scales(g, 0, PACK)
+            sort_codes(g, 2, 4)
         neg_aud = kept("neg_aud", [P, SG, PACK], F32)
-        nc.vector.tensor_scalar(out=neg_aud[:], in0=aud[:], scalar1=-1.0, scalar2=None, op0=ALU.mult)
+        nc.gpsimd.tensor_scalar(out=neg_aud[:], in0=aud[:], scalar1=-1.0, scalar2=0.0, op0=ALU.mult, op1=ALU.add)
         pos_aud = kept("pos_aud", [P, PACK * SG], F32)[:].rearrange("p (g t) -> p g t", t=PACK)
-        nc.vector.tensor_copy(out=pos_aud, in_=aud[:])
+        nc.gpsimd.tensor_copy(out=pos_aud, in_=aud[:])
 
         h_codes = [kept("h_codes%d" % u, [P, W], I32) for u in range(UNITS)]
         h_scales = [kept("h_scales%d" % u, [P, W], U8) for u in range(UNITS)]
         missed = {}
         h_slots = {}
         h_words = {}
-        open_out = {}
+        sums = {}
 
         def bank(b):
             return psum.tile([P, W], F32, name="bank%d" % b, tag="bank%d" % b)
+
+        warm_acc = bank(7)
+        for k in range(WARM):
+            nc.tensor.matmul_mx(
+                out=warm_acc[:],
+                lhsT=l_raw[0][:, 0, 0 : 2 * P].bitcast(FP4X4),
+                lhsT_scale=ls_first[:, 0, 0:P],
+                rhs=l_raw[0][:, 0, :].bitcast(FP4X4),
+                rhs_scale=ls_first[:, 0, :],
+                start=(k == 0),
+                stop=(k == WARM - 1),
+            )
 
         def reach(i):
             u, t = divmod(i, PACK)
@@ -144,7 +161,7 @@ def tile_campaign_reach_by_demographic_s4_kernel(
             u, t = divmod(i, PACK)
             g = u % SG
             if t == 0:
-                h_slots[u] = work.tile([P, PACK, W], BF16, name="h_slot", tag="h_slot", bufs=2, align_bytes=256)
+                h_slots[u] = work.tile([P, PACK, W], BF16, name="h_slot", tag="h_slot", bufs=3, align_bytes=256)
             if on_scalar:
                 nc.scalar.activation(
                     out=h_slots[u][:, t, :], in_=missed[i][:], func=ACT.Identity,
@@ -171,57 +188,73 @@ def tile_campaign_reach_by_demographic_s4_kernel(
                 in_=h_words[u][:, c0:c1, :].rearrange("p c t -> p (c t)"),
             )
 
-        def out_passes(j, b, g0, g1):
+        def out_passes(j, b, n0=0, n1=D):
             mb, c = divmod(j, W // P)
-            if g0 == 0:
-                open_out[j] = bank(b)
-            for g in range(g0, g1):
+            acc = bank(b)
+            for g in range(SG):
                 u = mb * SG + g
                 nc.tensor.matmul_mx(
-                    out=open_out[j][:],
+                    out=acc[:, 0 : n1 - n0],
                     lhsT=h_codes[u][:, P * c : P * (c + 1)].bitcast(FP8X4),
                     lhsT_scale=h_scales[u][:, P * c : P * (c + 1)],
-                    rhs=d_codes[:, g, :].bitcast(FP8X4),
-                    rhs_scale=d_scales[:, g, :],
+                    rhs=d_codes[:, g, n0:n1].bitcast(FP8X4),
+                    rhs_scale=d_scales[:, g, n0:n1],
                     start=(g == 0),
                     stop=(g == SG - 1),
                 )
+            sums[j, n0] = acc
 
-        def out_store(j, on_vector):
-            res = work.tile([P, D], F32, name="res", tag="res", bufs=4)
+        def out_store(j, on_vector, n0=0, n1=D):
+            res = work.tile([P, D], F32, name="res", tag="res", bufs=6)
             if on_vector:
-                nc.vector.tensor_copy(out=res[:], in_=open_out[j][:])
+                nc.vector.tensor_copy(out=res[:, 0 : n1 - n0], in_=sums[j, n0][:, 0 : n1 - n0])
             else:
-                nc.scalar.copy(out=res[:], in_=open_out[j][:])
-            nc.sync.dma_start(out=out[P * j : P * (j + 1), :], in_=res[:])
+                nc.scalar.copy(out=res[:, 0 : n1 - n0], in_=sums[j, n0][:, 0 : n1 - n0])
+            nc.sync.dma_start(out=out[P * j : P * (j + 1), n0:n1], in_=res[:, 0 : n1 - n0])
 
         done = 0
         for i in range(STEPS):
             u, t = divmod(i, PACK)
             reach(i)
-            if u < UNITS - 1:
+            if i < STEPS - ON_SCALAR:
                 weigh(i, False)
-            if u > 0 and t == 0:
+            if 0 < u < UNITS - 1 and t == 0:
                 interleave(u - 1, 0, W)
-            if u > 0 and t == 1:
+            if 0 < u < UNITS - 1 and t == (1 if u < UNITS - 2 else QT):
                 quantize(u - 1, 0, W)
             if i >= FIRST_OUT and (i - FIRST_OUT) % OUT_EVERY == 0 and i < STEPS - 1:
-                out_passes(done, Z_BANKS + done % 2, 0, SG)
+                out_passes(done, Z_BANKS + done % 2)
                 out_store(done, False)
                 done = done + 1
-        for i in range(STEPS - PACK, STEPS):
-            weigh(i, True)
         last = TILES - W // P
+        late = list(range(STEPS - ON_SCALAR, STEPS))
+        for i in late[:LEAD]:
+            weigh(i, True)
+        late = late[LEAD:]
         for j in range(done, last):
-            out_passes(j, Z_BANKS + j % 2, 0, SG)
+            out_passes(j, (Z_BANKS + j - done) % 8)
             out_store(j, False)
-        for j in range(last, TILES):
-            out_passes(j, j - last, 0, SG - 1)
-        interleave(UNITS - 1, 0, P)
+            for i in late[(j - done) * RATE : (j - done + 1) * RATE]:
+                weigh(i, True)
+        for i in late[(last - done) * RATE :]:
+            weigh(i, True)
+        u = UNITS - 1
+        interleave(u - 1, 0, W // 2)
+        interleave(u - 1, W // 2, W)
+        quantize(u - 1, 0, W // 2)
+        interleave(u, 0, P)
+        quantize(u - 1, W // 2, W)
         for c in range(W // P):
             if c + 1 < W // P:
-                interleave(UNITS - 1, P * (c + 1), P * (c + 2))
-            quantize(UNITS - 1, P * c, P * (c + 1))
-            out_passes(last + c, c, SG - 1, SG)
-        for j in range(last, TILES):
-            out_store(j, j == TILES - 1)
+                interleave(u, P * (c + 1), P * (c + 2))
+            quantize(u, P * c, P * (c + 1))
+            b = (Z_BANKS + last + c - done) % 8
+            if c + 1 < W // P:
+                out_passes(last + c, b)
+            else:
+                out_passes(last + c, b, 0, D // 2)
+                out_passes(last + c, (b + 1) % 8, D // 2, D)
+        for j in range(last, TILES - 1):
+            out_store(j, j == TILES - 2)
+        out_store(TILES - 1, False, 0, D // 2)
+        out_store(TILES - 1, True, D // 2, D)

@@ -2,8 +2,8 @@ from contextlib import ExitStack
 
 import concourse.mybir as mybir
 
-M, K, S, D = 2048, 1024, 1536, 512
-FLOPS = 2 * M * K * S + 2 * M * S * D
+PLANS, PLACEMENTS, SEGMENTS, CELLS = 2048, 1024, 1536, 512
+FLOPS = 2 * PLANS * PLACEMENTS * SEGMENTS + 2 * PLANS * SEGMENTS * CELLS
 
 F32 = mybir.dt.float32
 BF16 = mybir.dt.bfloat16
@@ -15,23 +15,27 @@ ACT = mybir.ActivationFunctionType
 ALU = mybir.AluOpType
 
 P = 128
-PACK = 4
-W = 512
-KG = K // W
-SG = S // W
-MB = M // W
-UNITS = MB * SG
-STEPS = UNITS * PACK
-TILES = M // P
+SLOTS = 4
+QUADS = 4
+GROUP = P * SLOTS
+BLOCK = 512
+K_GROUPS = PLACEMENTS // GROUP
+S_GROUPS = SEGMENTS // GROUP
+UNITS = (PLANS // BLOCK) * S_GROUPS
+STEPS = UNITS * SLOTS
+TILES = PLANS // P
+TILES_PER_BLOCK = BLOCK // P
+
+BANKS = 8
 Z_BANKS = 6
+WARM_PASSES = 3
 FIRST_OUT = 32
-OUT_EVERY = 3
-E_BUFS = 20
-WARM = 2
-ON_SCALAR = 4
-LEAD = 2
-RATE = 2
-QT = 3
+OUT_EVERY = STEPS // TILES
+MISSED_BUFS = 20
+SLOT_BUFS = 3
+WORD_BUFS = 2
+RESULT_BUFS = 12
+EARLY_TILES = 2
 
 
 def tile_campaign_reach_by_demographic_s4_kernel(
@@ -47,214 +51,221 @@ def tile_campaign_reach_by_demographic_s4_kernel(
         def kept(name, shape, dtype):
             return keep.tile(shape, dtype, name=name, align_bytes=256)
 
-        def plane(name, groups, width):
-            t = kept(name, [P, groups, width], U8)
-            nc.vector.memset(t[:].rearrange("p g n -> p (g n)").bitcast(I32), 0)
-            return t
+        def bank(b):
+            return psum.tile([P, BLOCK], F32, name="bank%d" % b, tag="bank%d" % b)
 
-        def load_scales(t, scales, col0, width, quads=range(4)):
+        def scale_plane(name, groups, width):
+            plane = kept(name, [P, groups, width], U8)
+            nc.vector.memset(plane[:].rearrange("p g n -> p (g n)").bitcast(I32), 0)
+            return plane
+
+        def load_scales(plane, scales, col0, col1, quads=range(QUADS)):
             for q in quads:
-                src = scales[:, 4 * q : 4 * q + 4, col0 : col0 + width].rearrange("g r n -> r g n")
-                nc.sync.dma_start(out=t[32 * q : 32 * q + 4, :, :].bitcast(I32), in_=src.bitcast(I32))
+                rows = scales[:, 4 * q : 4 * q + 4, col0:col1].rearrange("g r n -> r g n")
+                nc.sync.dma_start(out=plane[32 * q : 32 * q + 4, :, :].bitcast(I32), in_=rows.bitcast(I32))
 
         def load_fp4(name, words, j):
-            t = kept(name, [P, KG, 2 * W], U8)
-            src = words[:, :, 2 * W * j : 2 * W * (j + 1)].rearrange("g p n -> p g n")
-            nc.sync.dma_start(out=t[:].bitcast(I32), in_=src.bitcast(I32))
-            return t
+            codes = kept(name, [P, K_GROUPS, 2 * GROUP], U8)
+            cols = words[:, :, 2 * GROUP * j : 2 * GROUP * (j + 1)].rearrange("g p n -> p g n")
+            nc.sync.dma_start(out=codes[:].bitcast(I32), in_=cols.bitcast(I32))
+            return codes
 
-        warm = kept("warm", [P, 8], F32)
-        ls_first = plane("ls_first", KG, W)
-        as_first = plane("as_first", KG, W)
-        nc.vector.memset(warm[:, 0:1], 0.0)
-        nc.scalar.activation(out=warm[:, 4:5], in_=warm[:, 0:1], func=ACT.Exp)
-        ls_rest = plane("ls_rest", KG, S - W)
-        as_rest = plane("as_rest", KG, M - W)
-        d_scales = plane("d_scales", SG, D)
+        l_scales_first = scale_plane("l_scales_first", K_GROUPS, GROUP)
+        a_scales_first = scale_plane("a_scales_first", K_GROUPS, BLOCK)
+        l_scales_rest = scale_plane("l_scales_rest", K_GROUPS, SEGMENTS - GROUP)
+        a_scales_rest = scale_plane("a_scales_rest", K_GROUPS, PLANS - BLOCK)
+        d_scales = scale_plane("d_scales", S_GROUPS, CELLS)
 
-        load_scales(ls_first, lognon_scales, 0, W)
-        l_raw = [load_fp4("l_raw0", lognon_words, 0)]
-        load_scales(as_first, plans_scales, 0, W, range(0, 2))
+        l_codes = [load_fp4("l_codes0", lognon_words, 0)]
+        load_scales(l_scales_first, lognon_scales, 0, GROUP)
+        load_scales(a_scales_first, plans_scales, 0, BLOCK, range(0, QUADS // 2))
         a_codes = [load_fp4("a_codes0", plans_words, 0)]
-        load_scales(as_first, plans_scales, 0, W, range(2, 4))
-        l_raw.append(load_fp4("l_raw1", lognon_words, 1))
-        load_scales(ls_rest, lognon_scales, W, S - W)
-        l_raw.append(load_fp4("l_raw2", lognon_words, 2))
-        aud = kept("aud", [P, SG, PACK], BF16)
-        nc.sync.dma_start(out=aud[:], in_=audience.rearrange("(g p t) -> p g t", p=P, t=PACK))
-        load_scales(as_rest, plans_scales, W, M - W)
+        load_scales(a_scales_first, plans_scales, 0, BLOCK, range(QUADS // 2, QUADS))
+        l_codes.append(load_fp4("l_codes1", lognon_words, 1))
+        load_scales(l_scales_rest, lognon_scales, GROUP, SEGMENTS)
+        l_codes.append(load_fp4("l_codes2", lognon_words, 2))
+        aud = kept("aud", [P, S_GROUPS, SLOTS], BF16)
+        nc.sync.dma_start(out=aud[:], in_=audience.rearrange("(g p t) -> p g t", p=P, t=SLOTS))
+        load_scales(a_scales_rest, plans_scales, BLOCK, PLANS)
         a_codes.append(load_fp4("a_codes1", plans_words, 1))
-        load_scales(d_scales, demo_scales, 0, D)
-        d_codes = kept("d_codes", [P, SG, D], I32)
+        load_scales(d_scales, demo_scales, 0, CELLS)
+        d_codes = kept("d_codes", [P, S_GROUPS, CELLS], I32)
         nc.sync.dma_start(out=d_codes[:], in_=demo_words.rearrange("g p n t -> p g (n t)").bitcast(I32))
-        for j in range(2, MB):
-            a_codes.append(load_fp4("a_codes%d" % j, plans_words, j))
+        a_codes.append(load_fp4("a_codes2", plans_words, 2))
+        a_codes.append(load_fp4("a_codes3", plans_words, 3))
 
-        l_codes = [kept("l_codes%d" % g, [P, PACK, KG, 2 * P], U8) for g in range(SG)]
-        l_scales = [kept("l_scales%d" % g, [P, PACK, KG, P], U8) for g in range(SG)]
+        sorted_codes = [kept("sorted_codes%d" % g, [P, SLOTS, K_GROUPS, 2 * P], U8) for g in range(S_GROUPS)]
+        sorted_scales = [kept("sorted_scales%d" % g, [P, SLOTS, K_GROUPS, P], U8) for g in range(S_GROUPS)]
 
         def sort_codes(g, t0, t1):
-            src = l_raw[g][:].rearrange("p k (m t b) -> p t k m b", t=PACK, b=2)
-            dst = l_codes[g][:].rearrange("p t k (m b) -> p t k m b", b=2)
+            src = l_codes[g][:].rearrange("p k (m t b) -> p t k m b", t=SLOTS, b=2)
+            dst = sorted_codes[g][:].rearrange("p t k (m b) -> p t k m b", b=2)
             nc.vector.tensor_copy(out=dst[:, t0:t1], in_=src[:, t0:t1])
 
-        def sort_scales(g, t0, t1):
-            raw = ls_first[:] if g == 0 else ls_rest[:, :, W * (g - 1) : W * g]
-            src = raw.rearrange("p k (m t) -> p t k m", t=PACK)
-            nc.vector.tensor_copy(out=l_scales[g][:, t0:t1], in_=src[:, t0:t1])
+        def sort_scales(g):
+            plane = l_scales_first[:] if g == 0 else l_scales_rest[:, :, GROUP * (g - 1) : GROUP * g]
+            nc.vector.tensor_copy(out=sorted_scales[g][:], in_=plane.rearrange("p k (m t) -> p t k m", t=SLOTS))
 
-        sort_scales(0, 0, PACK)
-        sort_codes(0, 0, 1)
-        sort_codes(0, 1, 2)
-        sort_codes(0, 2, 4)
-        for g in range(1, SG):
-            sort_codes(g, 0, 2)
-            sort_scales(g, 0, PACK)
-            sort_codes(g, 2, 4)
-        neg_aud = kept("neg_aud", [P, SG, PACK], F32)
+        for g in range(S_GROUPS - 1):
+            sort_codes(g, 0, SLOTS // 2)
+            sort_scales(g)
+            sort_codes(g, SLOTS // 2, SLOTS)
+        sort_codes(S_GROUPS - 1, 0, SLOTS)
+        sort_scales(S_GROUPS - 1)
+
+        neg_aud = kept("neg_aud", [P, S_GROUPS, SLOTS], F32)
         nc.gpsimd.tensor_scalar(out=neg_aud[:], in0=aud[:], scalar1=-1.0, scalar2=0.0, op0=ALU.mult, op1=ALU.add)
-        pos_aud = kept("pos_aud", [P, PACK * SG], F32)[:].rearrange("p (g t) -> p g t", t=PACK)
-        nc.gpsimd.tensor_copy(out=pos_aud, in_=aud[:])
+        pos_aud = kept("pos_aud", [P, S_GROUPS, SLOTS], F32)
+        nc.gpsimd.tensor_copy(out=pos_aud[:], in_=aud[:])
 
-        h_codes = [kept("h_codes%d" % u, [P, W], I32) for u in range(UNITS)]
-        h_scales = [kept("h_scales%d" % u, [P, W], U8) for u in range(UNITS)]
+        warm = bank(BANKS - 1)
+        for n in range(WARM_PASSES):
+            nc.tensor.matmul_mx(
+                out=warm[:],
+                lhsT=l_codes[0][:, 0, 0 : 2 * P].bitcast(FP4X4),
+                lhsT_scale=l_scales_first[:, 0, 0:P],
+                rhs=l_codes[0][:, 0, :].bitcast(FP4X4),
+                rhs_scale=l_scales_first[:, 0, :],
+                start=(n == 0),
+                stop=(n == WARM_PASSES - 1),
+            )
+
+        h_codes = [kept("h_codes%d" % u, [P, BLOCK], I32) for u in range(UNITS)]
+        h_scales = [kept("h_scales%d" % u, [P, BLOCK], U8) for u in range(UNITS)]
         missed = {}
         h_slots = {}
         h_words = {}
         sums = {}
 
-        def bank(b):
-            return psum.tile([P, W], F32, name="bank%d" % b, tag="bank%d" % b)
-
-        warm_acc = bank(7)
-        for k in range(WARM):
-            nc.tensor.matmul_mx(
-                out=warm_acc[:],
-                lhsT=l_raw[0][:, 0, 0 : 2 * P].bitcast(FP4X4),
-                lhsT_scale=ls_first[:, 0, 0:P],
-                rhs=l_raw[0][:, 0, :].bitcast(FP4X4),
-                rhs_scale=ls_first[:, 0, :],
-                start=(k == 0),
-                stop=(k == WARM - 1),
-            )
-
-        def reach(i):
-            u, t = divmod(i, PACK)
-            mb, g = divmod(u, SG)
-            z = bank(i % Z_BANKS)
-            for k in range(KG):
-                a_scale = as_first[:, k, :] if mb == 0 else as_rest[:, k, W * (mb - 1) : W * mb]
+        def stage_one(step):
+            unit, t = divmod(step, SLOTS)
+            block, g = divmod(unit, S_GROUPS)
+            z = bank(step % Z_BANKS)
+            for k in range(K_GROUPS):
+                if block == 0:
+                    a_scales = a_scales_first[:, k, :]
+                else:
+                    a_scales = a_scales_rest[:, k, BLOCK * (block - 1) : BLOCK * block]
                 nc.tensor.matmul_mx(
                     out=z[:],
-                    lhsT=l_codes[g][:, t, k, :].bitcast(FP4X4),
-                    lhsT_scale=l_scales[g][:, t, k, :],
-                    rhs=a_codes[mb][:, k, :].bitcast(FP4X4),
-                    rhs_scale=a_scale,
+                    lhsT=sorted_codes[g][:, t, k, :].bitcast(FP4X4),
+                    lhsT_scale=sorted_scales[g][:, t, k, :],
+                    rhs=a_codes[block][:, k, :].bitcast(FP4X4),
+                    rhs_scale=a_scales,
                     start=(k == 0),
-                    stop=(k == KG - 1),
+                    stop=(k == K_GROUPS - 1),
                 )
-            e = work.tile([P, W], F32, name="e", tag="e", bufs=E_BUFS)
-            nc.scalar.activation(out=e[:], in_=z[:], func=ACT.Exp)
-            missed[i] = e
+            missed[step] = work.tile([P, BLOCK], F32, name="missed", tag="missed", bufs=MISSED_BUFS)
+            nc.scalar.activation(out=missed[step][:], in_=z[:], func=ACT.Exp)
 
-        def weigh(i, on_scalar):
-            u, t = divmod(i, PACK)
-            g = u % SG
+        def weigh(step, on_scalar):
+            unit, t = divmod(step, SLOTS)
+            g = unit % S_GROUPS
             if t == 0:
-                h_slots[u] = work.tile([P, PACK, W], BF16, name="h_slot", tag="h_slot", bufs=3, align_bytes=256)
+                h_slots[unit] = work.tile(
+                    [P, SLOTS, BLOCK], BF16, name="h_slot", tag="h_slot", bufs=SLOT_BUFS, align_bytes=256
+                )
             if on_scalar:
                 nc.scalar.activation(
-                    out=h_slots[u][:, t, :], in_=missed[i][:], func=ACT.Identity,
-                    scale=neg_aud[:, g, t : t + 1], bias=pos_aud[:, g, t : t + 1],
+                    out=h_slots[unit][:, t, :],
+                    in_=missed[step][:],
+                    func=ACT.Identity,
+                    scale=neg_aud[:, g, t : t + 1],
+                    bias=pos_aud[:, g, t : t + 1],
                 )
             else:
                 nc.vector.tensor_scalar(
-                    out=h_slots[u][:, t, :], in0=missed[i][:], scalar1=-1.0, scalar2=neg_aud[:, g, t : t + 1],
-                    op0=ALU.add, op1=ALU.mult,
+                    out=h_slots[unit][:, t, :],
+                    in0=missed[step][:],
+                    scalar1=-1.0,
+                    scalar2=neg_aud[:, g, t : t + 1],
+                    op0=ALU.add,
+                    op1=ALU.mult,
                 )
 
-        def interleave(u, c0, c1):
+        def interleave(unit, c0=0, c1=BLOCK):
             if c0 == 0:
-                h_words[u] = work.tile([P, W, PACK], BF16, name="h_word", tag="h_word", bufs=2, align_bytes=256)
+                h_words[unit] = work.tile(
+                    [P, BLOCK, SLOTS], BF16, name="h_word", tag="h_word", bufs=WORD_BUFS, align_bytes=256
+                )
             nc.vector.tensor_copy(
-                out=h_words[u][:, c0:c1, :].rearrange("p (c i) t -> p c t i", i=4),
-                in_=h_slots[u][:, :, c0:c1].rearrange("p t (c i) -> p c t i", i=4),
+                out=h_words[unit][:, c0:c1, :].rearrange("p (c i) t -> p c t i", i=4),
+                in_=h_slots[unit][:, :, c0:c1].rearrange("p t (c i) -> p c t i", i=4),
             )
 
-        def quantize(u, c0, c1):
+        def quantize(unit, c0=0, c1=BLOCK):
             nc.vector.quantize_mx(
-                out=h_codes[u][:, c0:c1].bitcast(FP8X4),
-                scales=h_scales[u][:, c0:c1],
-                in_=h_words[u][:, c0:c1, :].rearrange("p c t -> p (c t)"),
+                out=h_codes[unit][:, c0:c1].bitcast(FP8X4),
+                scales=h_scales[unit][:, c0:c1],
+                in_=h_words[unit][:, c0:c1, :].rearrange("p c t -> p (c t)"),
             )
 
-        def out_passes(j, b, n0=0, n1=D):
-            mb, c = divmod(j, W // P)
-            acc = bank(b)
-            for g in range(SG):
-                u = mb * SG + g
+        def stage_two(tile, b, groups=range(S_GROUPS), n0=0, n1=CELLS):
+            block, c = divmod(tile, TILES_PER_BLOCK)
+            for g in groups:
+                if g == 0:
+                    sums[tile, n0] = bank(b)
+                unit = block * S_GROUPS + g
                 nc.tensor.matmul_mx(
-                    out=acc[:, 0 : n1 - n0],
-                    lhsT=h_codes[u][:, P * c : P * (c + 1)].bitcast(FP8X4),
-                    lhsT_scale=h_scales[u][:, P * c : P * (c + 1)],
+                    out=sums[tile, n0][:, 0 : n1 - n0],
+                    lhsT=h_codes[unit][:, P * c : P * (c + 1)].bitcast(FP8X4),
+                    lhsT_scale=h_scales[unit][:, P * c : P * (c + 1)],
                     rhs=d_codes[:, g, n0:n1].bitcast(FP8X4),
                     rhs_scale=d_scales[:, g, n0:n1],
                     start=(g == 0),
-                    stop=(g == SG - 1),
+                    stop=(g == S_GROUPS - 1),
                 )
-            sums[j, n0] = acc
 
-        def out_store(j, on_vector, n0=0, n1=D):
-            res = work.tile([P, D], F32, name="res", tag="res", bufs=6)
+        def store(tile, on_vector=False, n0=0, n1=CELLS):
+            result = work.tile([P, CELLS], F32, name="result", tag="result", bufs=RESULT_BUFS)
             if on_vector:
-                nc.vector.tensor_copy(out=res[:, 0 : n1 - n0], in_=sums[j, n0][:, 0 : n1 - n0])
+                nc.vector.tensor_copy(out=result[:, 0 : n1 - n0], in_=sums[tile, n0][:, 0 : n1 - n0])
             else:
-                nc.scalar.copy(out=res[:, 0 : n1 - n0], in_=sums[j, n0][:, 0 : n1 - n0])
-            nc.sync.dma_start(out=out[P * j : P * (j + 1), n0:n1], in_=res[:, 0 : n1 - n0])
+                nc.scalar.copy(out=result[:, 0 : n1 - n0], in_=sums[tile, n0][:, 0 : n1 - n0])
+            nc.sync.dma_start(out=out[P * tile : P * (tile + 1), n0:n1], in_=result[:, 0 : n1 - n0])
 
+        last_unit = UNITS - 1
         done = 0
-        for i in range(STEPS):
-            u, t = divmod(i, PACK)
-            reach(i)
-            if i < STEPS - ON_SCALAR:
-                weigh(i, False)
-            if 0 < u < UNITS - 1 and t == 0:
-                interleave(u - 1, 0, W)
-            if 0 < u < UNITS - 1 and t == (1 if u < UNITS - 2 else QT):
-                quantize(u - 1, 0, W)
-            if i >= FIRST_OUT and (i - FIRST_OUT) % OUT_EVERY == 0 and i < STEPS - 1:
-                out_passes(done, Z_BANKS + done % 2)
-                out_store(done, False)
+        for step in range(STEPS):
+            unit, t = divmod(step, SLOTS)
+            stage_one(step)
+            if unit < last_unit:
+                weigh(step, on_scalar=False)
+                if unit > 0 and t == 1:
+                    interleave(unit - 1)
+                if unit > 0 and t == SLOTS - 1:
+                    quantize(unit - 1)
+            if FIRST_OUT <= step < STEPS - 1 and (step - FIRST_OUT) % OUT_EVERY == 0:
+                stage_two(done, Z_BANKS + done % (BANKS - Z_BANKS))
+                store(done)
                 done = done + 1
-        last = TILES - W // P
-        late = list(range(STEPS - ON_SCALAR, STEPS))
-        for i in late[:LEAD]:
-            weigh(i, True)
-        late = late[LEAD:]
-        for j in range(done, last):
-            out_passes(j, (Z_BANKS + j - done) % 8)
-            out_store(j, False)
-            for i in late[(j - done) * RATE : (j - done + 1) * RATE]:
-                weigh(i, True)
-        for i in late[(last - done) * RATE :]:
-            weigh(i, True)
-        u = UNITS - 1
-        interleave(u - 1, 0, W // 2)
-        interleave(u - 1, W // 2, W)
-        quantize(u - 1, 0, W // 2)
-        interleave(u, 0, P)
-        quantize(u - 1, W // 2, W)
-        for c in range(W // P):
-            if c + 1 < W // P:
-                interleave(u, P * (c + 1), P * (c + 2))
-            quantize(u, P * c, P * (c + 1))
-            b = (Z_BANKS + last + c - done) % 8
-            if c + 1 < W // P:
-                out_passes(last + c, b)
-            else:
-                out_passes(last + c, b, 0, D // 2)
-                out_passes(last + c, (b + 1) % 8, D // 2, D)
-        for j in range(last, TILES - 1):
-            out_store(j, j == TILES - 2)
-        out_store(TILES - 1, False, 0, D // 2)
-        out_store(TILES - 1, True, D // 2, D)
+
+        for step in range(STEPS - SLOTS, STEPS):
+            weigh(step, on_scalar=True)
+        last_block = TILES - TILES_PER_BLOCK
+        for tile in range(done, last_block):
+            stage_two(tile, (Z_BANKS + tile - done) % BANKS)
+            store(tile)
+
+        half, quarter = CELLS // 2, CELLS // 4
+        pieces = [(tile, 0, CELLS) for tile in range(last_block, TILES - 2)]
+        pieces = pieces + [(TILES - 2, 0, half), (TILES - 2, half, CELLS), (TILES - 1, 0, half)]
+        pieces = pieces + [(TILES - 1, half, half + quarter), (TILES - 1, half + quarter, CELLS)]
+        first_bank = Z_BANKS + last_block - done
+        for n, (tile, n0, n1) in enumerate(pieces[:EARLY_TILES]):
+            stage_two(tile, (first_bank + n) % BANKS, range(1), n0, n1)
+
+        interleave(last_unit - 1, 0, 2 * P)
+        interleave(last_unit, 0, 2 * P)
+        quantize(last_unit - 1, 0, 2 * P)
+        quantize(last_unit, 0, 2 * P)
+        interleave(last_unit - 1, 2 * P, BLOCK)
+        interleave(last_unit, 2 * P, 3 * P)
+        quantize(last_unit - 1, 2 * P, BLOCK)
+        interleave(last_unit, 3 * P, BLOCK)
+        quantize(last_unit, 2 * P, 3 * P)
+        quantize(last_unit, 3 * P, BLOCK)
+
+        for n, (tile, n0, n1) in enumerate(pieces):
+            stage_two(tile, (first_bank + n) % BANKS, range(1 if n < EARLY_TILES else 0, S_GROUPS), n0, n1)
+            store(tile, n0 == half, n0, n1)

@@ -28,7 +28,6 @@ TILES_PER_BLOCK = BLOCK // P
 
 BANKS = 8
 Z_BANKS = 6
-WARM_PASSES = 3
 FIRST_OUT = 32
 OUT_EVERY = STEPS // TILES
 MISSED_BUFS = 20
@@ -117,18 +116,6 @@ def tile_campaign_reach_by_demographic_s4_kernel(
         nc.gpsimd.tensor_scalar(out=neg_aud[:], in0=aud[:], scalar1=-1.0, scalar2=0.0, op0=ALU.mult, op1=ALU.add)
         pos_aud = kept("pos_aud", [P, S_GROUPS, SLOTS], F32)
         nc.gpsimd.tensor_copy(out=pos_aud[:], in_=aud[:])
-
-        warm = bank(BANKS - 1)
-        for n in range(WARM_PASSES):
-            nc.tensor.matmul_mx(
-                out=warm[:],
-                lhsT=l_codes[0][:, 0, 0 : 2 * P].bitcast(FP4X4),
-                lhsT_scale=l_scales_first[:, 0, 0:P],
-                rhs=l_codes[0][:, 0, :].bitcast(FP4X4),
-                rhs_scale=l_scales_first[:, 0, :],
-                start=(n == 0),
-                stop=(n == WARM_PASSES - 1),
-            )
 
         h_codes = [kept("h_codes%d" % u, [P, BLOCK], I32) for u in range(UNITS)]
         h_scales = [kept("h_scales%d" % u, [P, BLOCK], U8) for u in range(UNITS)]

from contextlib import ExitStack

import concourse.mybir as mybir

PLANS, PLACEMENTS, SEGMENTS, CELLS = 2048, 1024, 1536, 512
FLOPS = 2 * PLANS * PLACEMENTS * SEGMENTS + 2 * PLANS * SEGMENTS * CELLS

F32 = mybir.dt.float32
BF16 = mybir.dt.bfloat16
I32 = mybir.dt.int32
U8 = mybir.dt.uint8
FP8X4 = mybir.dt.float8_e4m3fn_x4
FP4X4 = mybir.dt.float4_e2m1fn_x4
ACT = mybir.ActivationFunctionType
ALU = mybir.AluOpType

P = 128
SLOTS = 4
QUADS = 4
GROUP = P * SLOTS
BLOCK = 512
K_GROUPS = PLACEMENTS // GROUP
S_GROUPS = SEGMENTS // GROUP
UNITS = (PLANS // BLOCK) * S_GROUPS
STEPS = UNITS * SLOTS
TILES = PLANS // P
TILES_PER_BLOCK = BLOCK // P

BANKS = 8
Z_BANKS = 6
FIRST_OUT = 32
OUT_EVERY = STEPS // TILES
MISSED_BUFS = 20
SLOT_BUFS = 3
WORD_BUFS = 2
RESULT_BUFS = 12
EARLY_TILES = 2


def tile_campaign_reach_by_demographic_s4_kernel(
    tc, plans_words, plans_scales, lognon_words, lognon_scales, audience, demo_words, demo_scales, out
):
    nc = tc.nc
    with ExitStack() as ctx:
        keep = ctx.enter_context(tc.tile_pool(name="keep", bufs=1))
        work = ctx.enter_context(tc.tile_pool(name="work", bufs=1))
        psum = ctx.enter_context(tc.psum_pool(name="psum", bufs=1))
        ctx.enter_context(tc.manual_schedule())

        def kept(name, shape, dtype):
            return keep.tile(shape, dtype, name=name, align_bytes=256)

        def bank(b):
            return psum.tile([P, BLOCK], F32, name="bank%d" % b, tag="bank%d" % b)

        def scale_plane(name, groups, width):
            plane = kept(name, [P, groups, width], U8)
            nc.vector.memset(plane[:].rearrange("p g n -> p (g n)").bitcast(I32), 0)
            return plane

        def load_scales(plane, scales, col0, col1, quads=range(QUADS)):
            for q in quads:
                rows = scales[:, 4 * q : 4 * q + 4, col0:col1].rearrange("g r n -> r g n")
                nc.sync.dma_start(out=plane[32 * q : 32 * q + 4, :, :].bitcast(I32), in_=rows.bitcast(I32))

        def load_fp4(name, words, j):
            codes = kept(name, [P, K_GROUPS, 2 * GROUP], U8)
            cols = words[:, :, 2 * GROUP * j : 2 * GROUP * (j + 1)].rearrange("g p n -> p g n")
            nc.sync.dma_start(out=codes[:].bitcast(I32), in_=cols.bitcast(I32))
            return codes

        l_scales_first = scale_plane("l_scales_first", K_GROUPS, GROUP)
        a_scales_first = scale_plane("a_scales_first", K_GROUPS, BLOCK)
        l_scales_rest = scale_plane("l_scales_rest", K_GROUPS, SEGMENTS - GROUP)
        a_scales_rest = scale_plane("a_scales_rest", K_GROUPS, PLANS - BLOCK)
        d_scales = scale_plane("d_scales", S_GROUPS, CELLS)

        l_codes = [load_fp4("l_codes0", lognon_words, 0)]
        load_scales(l_scales_first, lognon_scales, 0, GROUP)
        load_scales(a_scales_first, plans_scales, 0, BLOCK, range(0, QUADS // 2))
        a_codes = [load_fp4("a_codes0", plans_words, 0)]
        load_scales(a_scales_first, plans_scales, 0, BLOCK, range(QUADS // 2, QUADS))
        l_codes.append(load_fp4("l_codes1", lognon_words, 1))
        load_scales(l_scales_rest, lognon_scales, GROUP, SEGMENTS)
        l_codes.append(load_fp4("l_codes2", lognon_words, 2))
        aud = kept("aud", [P, S_GROUPS, SLOTS], BF16)
        nc.sync.dma_start(out=aud[:], in_=audience.rearrange("(g p t) -> p g t", p=P, t=SLOTS))
        load_scales(a_scales_rest, plans_scales, BLOCK, PLANS)
        a_codes.append(load_fp4("a_codes1", plans_words, 1))
        load_scales(d_scales, demo_scales, 0, CELLS)
        d_codes = kept("d_codes", [P, S_GROUPS, CELLS], I32)
        nc.sync.dma_start(out=d_codes[:], in_=demo_words.rearrange("g p n t -> p g (n t)").bitcast(I32))
        a_codes.append(load_fp4("a_codes2", plans_words, 2))
        a_codes.append(load_fp4("a_codes3", plans_words, 3))

        sorted_codes = [kept("sorted_codes%d" % g, [P, SLOTS, K_GROUPS, 2 * P], U8) for g in range(S_GROUPS)]
        sorted_scales = [kept("sorted_scales%d" % g, [P, SLOTS, K_GROUPS, P], U8) for g in range(S_GROUPS)]

        def sort_codes(g, t0, t1):
            src = l_codes[g][:].rearrange("p k (m t b) -> p t k m b", t=SLOTS, b=2)
            dst = sorted_codes[g][:].rearrange("p t k (m b) -> p t k m b", b=2)
            nc.vector.tensor_copy(out=dst[:, t0:t1], in_=src[:, t0:t1])

        def sort_scales(g):
            plane = l_scales_first[:] if g == 0 else l_scales_rest[:, :, GROUP * (g - 1) : GROUP * g]
            nc.vector.tensor_copy(out=sorted_scales[g][:], in_=plane.rearrange("p k (m t) -> p t k m", t=SLOTS))

        for g in range(S_GROUPS - 1):
            sort_codes(g, 0, SLOTS // 2)
            sort_scales(g)
            sort_codes(g, SLOTS // 2, SLOTS)
        sort_codes(S_GROUPS - 1, 0, SLOTS)
        sort_scales(S_GROUPS - 1)

        neg_aud = kept("neg_aud", [P, S_GROUPS, SLOTS], F32)
        nc.gpsimd.tensor_scalar(out=neg_aud[:], in0=aud[:], scalar1=-1.0, scalar2=0.0, op0=ALU.mult, op1=ALU.add)
        pos_aud = kept("pos_aud", [P, S_GROUPS, SLOTS], F32)
        nc.gpsimd.tensor_copy(out=pos_aud[:], in_=aud[:])

        h_codes = [kept("h_codes%d" % u, [P, BLOCK], I32) for u in range(UNITS)]
        h_scales = [kept("h_scales%d" % u, [P, BLOCK], U8) for u in range(UNITS)]
        missed = {}
        h_slots = {}
        h_words = {}
        sums = {}

        def stage_one(step):
            unit, t = divmod(step, SLOTS)
            block, g = divmod(unit, S_GROUPS)
            z = bank(step % Z_BANKS)
            for k in range(K_GROUPS):
                if block == 0:
                    a_scales = a_scales_first[:, k, :]
                else:
                    a_scales = a_scales_rest[:, k, BLOCK * (block - 1) : BLOCK * block]
                nc.tensor.matmul_mx(
                    out=z[:],
                    lhsT=sorted_codes[g][:, t, k, :].bitcast(FP4X4),
                    lhsT_scale=sorted_scales[g][:, t, k, :],
                    rhs=a_codes[block][:, k, :].bitcast(FP4X4),
                    rhs_scale=a_scales,
                    start=(k == 0),
                    stop=(k == K_GROUPS - 1),
                )
            missed[step] = work.tile([P, BLOCK], F32, name="missed", tag="missed", bufs=MISSED_BUFS)
            nc.scalar.activation(out=missed[step][:], in_=z[:], func=ACT.Exp)

        def weigh(step, on_scalar):
            unit, t = divmod(step, SLOTS)
            g = unit % S_GROUPS
            if t == 0:
                h_slots[unit] = work.tile(
                    [P, SLOTS, BLOCK], BF16, name="h_slot", tag="h_slot", bufs=SLOT_BUFS, align_bytes=256
                )
            if on_scalar:
                nc.scalar.activation(
                    out=h_slots[unit][:, t, :],
                    in_=missed[step][:],
                    func=ACT.Identity,
                    scale=neg_aud[:, g, t : t + 1],
                    bias=pos_aud[:, g, t : t + 1],
                )
            else:
                nc.vector.tensor_scalar(
                    out=h_slots[unit][:, t, :],
                    in0=missed[step][:],
                    scalar1=-1.0,
                    scalar2=neg_aud[:, g, t : t + 1],
                    op0=ALU.add,
                    op1=ALU.mult,
                )

        def interleave(unit, c0=0, c1=BLOCK):
            if c0 == 0:
                h_words[unit] = work.tile(
                    [P, BLOCK, SLOTS], BF16, name="h_word", tag="h_word", bufs=WORD_BUFS, align_bytes=256
                )
            nc.vector.tensor_copy(
                out=h_words[unit][:, c0:c1, :].rearrange("p (c i) t -> p c t i", i=4),
                in_=h_slots[unit][:, :, c0:c1].rearrange("p t (c i) -> p c t i", i=4),
            )

        def quantize(unit, c0=0, c1=BLOCK):
            nc.vector.quantize_mx(
                out=h_codes[unit][:, c0:c1].bitcast(FP8X4),
                scales=h_scales[unit][:, c0:c1],
                in_=h_words[unit][:, c0:c1, :].rearrange("p c t -> p (c t)"),
            )

        def stage_two(tile, b, groups=range(S_GROUPS), n0=0, n1=CELLS):
            block, c = divmod(tile, TILES_PER_BLOCK)
            for g in groups:
                if g == 0:
                    sums[tile, n0] = bank(b)
                unit = block * S_GROUPS + g
                nc.tensor.matmul_mx(
                    out=sums[tile, n0][:, 0 : n1 - n0],
                    lhsT=h_codes[unit][:, P * c : P * (c + 1)].bitcast(FP8X4),
                    lhsT_scale=h_scales[unit][:, P * c : P * (c + 1)],
                    rhs=d_codes[:, g, n0:n1].bitcast(FP8X4),
                    rhs_scale=d_scales[:, g, n0:n1],
                    start=(g == 0),
                    stop=(g == S_GROUPS - 1),
                )

        def store(tile, on_vector=False, n0=0, n1=CELLS):
            result = work.tile([P, CELLS], F32, name="result", tag="result", bufs=RESULT_BUFS)
            if on_vector:
                nc.vector.tensor_copy(out=result[:, 0 : n1 - n0], in_=sums[tile, n0][:, 0 : n1 - n0])
            else:
                nc.scalar.copy(out=result[:, 0 : n1 - n0], in_=sums[tile, n0][:, 0 : n1 - n0])
            nc.sync.dma_start(out=out[P * tile : P * (tile + 1), n0:n1], in_=result[:, 0 : n1 - n0])

        last_unit = UNITS - 1
        done = 0
        for step in range(STEPS):
            unit, t = divmod(step, SLOTS)
            stage_one(step)
            if unit < last_unit:
                weigh(step, on_scalar=False)
                if unit > 0 and t == 1:
                    interleave(unit - 1)
                if unit > 0 and t == SLOTS - 1:
                    quantize(unit - 1)
            if FIRST_OUT <= step < STEPS - 1 and (step - FIRST_OUT) % OUT_EVERY == 0:
                stage_two(done, Z_BANKS + done % (BANKS - Z_BANKS))
                store(done)
                done = done + 1

        for step in range(STEPS - SLOTS, STEPS):
            weigh(step, on_scalar=True)
        last_block = TILES - TILES_PER_BLOCK
        for tile in range(done, last_block):
            stage_two(tile, (Z_BANKS + tile - done) % BANKS)
            store(tile)

        half, quarter = CELLS // 2, CELLS // 4
        pieces = [(tile, 0, CELLS) for tile in range(last_block, TILES - 2)]
        pieces = pieces + [(TILES - 2, 0, half), (TILES - 2, half, CELLS), (TILES - 1, 0, half)]
        pieces = pieces + [(TILES - 1, half, half + quarter), (TILES - 1, half + quarter, CELLS)]
        first_bank = Z_BANKS + last_block - done
        for n, (tile, n0, n1) in enumerate(pieces[:EARLY_TILES]):
            stage_two(tile, (first_bank + n) % BANKS, range(1), n0, n1)

        interleave(last_unit - 1, 0, 2 * P)
        interleave(last_unit, 0, 2 * P)
        quantize(last_unit - 1, 0, 2 * P)
        quantize(last_unit, 0, 2 * P)
        interleave(last_unit - 1, 2 * P, BLOCK)
        interleave(last_unit, 2 * P, 3 * P)
        quantize(last_unit - 1, 2 * P, BLOCK)
        interleave(last_unit, 3 * P, BLOCK)
        quantize(last_unit, 2 * P, 3 * P)
        quantize(last_unit, 3 * P, BLOCK)

        for n, (tile, n0, n1) in enumerate(pieces):
            stage_two(tile, (first_bank + n) % BANKS, range(1 if n < EARLY_TILES else 0, S_GROUPS), n0, n1)
            store(tile, n0 == half, n0, n1)
